import numpy as np
import ml_dtypes


def mxq(x, axis, fmt="e4m3"):
    dtype, down = {"e4m3": (ml_dtypes.float8_e4m3fn, 7), "e5m2": (ml_dtypes.float8_e5m2, 14)}[fmt]
    v = np.moveaxis(np.asarray(x, np.float32).astype(ml_dtypes.bfloat16).astype(np.float64), axis, -1)
    blocks = v.reshape(v.shape[:-1] + (-1, 32))
    amax = np.abs(blocks).max(-1, keepdims=True)
    byte = np.maximum(np.where(amax > 0, np.frexp(amax)[1] - 1 + 127, 0) - down, 1)
    scale = np.exp2(byte - 127.0)
    codes = (blocks / scale).astype(np.float32).astype(dtype).astype(np.float64)
    return np.moveaxis((codes * scale).reshape(v.shape), -1, axis)


WIDE = False


def mx_kscale(k):
    if not WIDE:
        return np.ones(k)
    levels = np.array([10, -10, 5, -5, 0])
    if k % 512:
        return np.exp2(np.random.permutation(np.resize(levels, k // 32))).repeat(32)
    a = np.empty((k // 512, 16))
    for p in range(k // 512):
        a[p, :8] = np.random.permutation(np.resize(levels, 8))
        for g in range(8):
            far = levels[np.abs(levels - a[p, g]) >= 10]
            a[p, g + 8] = far[np.random.randint(len(far))]
    return np.exp2(a.ravel()).repeat(32)


def f64(x):
    return np.asarray(x).astype(np.float64)


def striped(idx):
    return np.tile(idx.reshape(-1, 16).T, (8, 1)).astype(np.uint16)


def unstriped(offs):
    return offs[:16].T.reshape(-1).astype(np.int64)


E2M1 = np.array([0.0, 0.5, 1.0, 1.5, 2.0, 3.0, 4.0, 6.0, -0.0, -0.5, -1.0, -1.5, -2.0, -3.0, -4.0, -6.0])


def pack_weight(w, fmt):
    k, n = w.shape
    w = f64(np.asarray(w, np.float32).astype(ml_dtypes.bfloat16)).reshape(k // 32, 32, n)
    amax = np.abs(w).max(1)
    if fmt == "e4m3":
        byte = np.frexp(amax)[1] - 1 + 127 - 7
    else:
        mant, ex = np.frexp(amax / 6.0)
        byte = np.where(mant > 0.5, ex, ex - 1) + 127
    byte = np.clip(np.where(amax > 0, byte, 1), 1, 254)
    scaled = (w * np.exp2(127.0 - byte)[:, None, :]).reshape(k, n).astype(np.float32)
    by_word = np.ascontiguousarray(scaled.reshape(k // 512, 128, 4, n).transpose(0, 1, 3, 2))
    if fmt == "e4m3":
        words = by_word.astype(ml_dtypes.float8_e4m3fn).view(np.uint8)
    else:
        c = by_word.astype(ml_dtypes.float4_e2m1fn).view(np.uint8) & 0xF
        words = (c[..., 0::2] | (c[..., 1::2] << 4)).reshape(k // 512, 128, 2 * n)
    return np.ascontiguousarray(words), np.ascontiguousarray(byte.astype(np.uint8).reshape(k // 512, 16, n))


def unpack_weight(words, scales, fmt):
    g, _, n = scales.shape
    words = np.ascontiguousarray(words).reshape(g, 128, n, -1)
    if fmt == "e4m3":
        vals = words.view(ml_dtypes.float8_e4m3fn).astype(np.float64)
    else:
        nib = np.empty((g, 128, n, 4), np.uint8)
        nib[..., 0::2] = words & 0xF
        nib[..., 1::2] = words >> 4
        vals = E2M1[nib]
    vals = vals * np.repeat(np.exp2(scales.astype(np.float64) - 127.0), 8, axis=1)[..., None]
    return vals.transpose(0, 1, 3, 2).reshape(g * 512, n)


def gelu(v):
    return 0.5 * v * (1.0 + np.tanh(np.sqrt(2.0 / np.pi) * (v + 0.044715 * v**3)))


def bf(x):
    return np.asarray(x, np.float32).astype(ml_dtypes.bfloat16)


def planes(Y):
    n, m = Y.shape
    b = f64(bf(Y)).reshape(n // 32, 32, m)
    amax = np.abs(b).max(1)
    byte = np.clip(np.where(amax > 0, np.frexp(amax)[1] - 1 + 127 - 7, 1), 1, 254)
    codes = (b * np.exp2(127.0 - byte)[:, None, :]).reshape(n, m).astype(np.float32).astype(ml_dtypes.float8_e4m3fn).view(np.uint8)
    words = codes.reshape(n // 512, 128, 4, m).transpose(0, 1, 3, 2)
    return np.ascontiguousarray(words), np.ascontiguousarray(byte.astype(np.uint8).reshape(n // 512, 16, m))


K, T, S, H, T2, P, N = 1536, 2048, 1024, 1024, 2048, 1024, 512

def setup_inputs():
    n = np.random.standard_normal
    s = mx_kscale(K)[:, None]
    u = mx_kscale(H)[:, None]
    d = {}
    d["tab_words"], d["tab_scales"] = pack_weight(n((K, T)) * s, "e4m3")
    d["offs"] = striped(np.random.permutation(T)[:S])
    d["w1"] = (n((K, H)) / K**0.5 / s * u.T).astype(np.float32)
    d["al"] = np.random.uniform(-0.6, 0.6, H).astype(np.float32)
    d["page0"] = (n((H, T2)) * u).astype(np.float32)
    d["wgs"] = np.exp(0.3 * n((128, S))).astype(np.float32)
    d["offs2"] = striped(np.random.permutation(T2)[:S])
    d["offs3"] = striped(np.random.permutation(T2)[:P])
    d["b"] = (0.5 * n(H) * u[:, 0]).astype(np.float32)
    d["w2_words"], d["w2_scales"] = pack_weight(n((H, N)) / H**0.5 / u, "e2m1")
    d["w3"] = (1.3 * n((H, N)) / H**0.5 / u).astype(np.float32)
    return d

def reference(tab_words, tab_scales, offs, w1, al, page0, wgs, offs2, offs3, b, w2_words, w2_scales, w3):
    v = unpack_weight(tab_words, tab_scales, "e4m3")[:, unstriped(offs)]
    day = mxq(f64(w1), 0, "e4m3").T @ v
    h = np.maximum(day, f64(al)[:, None] * day)
    page = f64(page0).copy()
    page[:, unstriped(offs2)] = np.tile(f64(wgs), (H // 128, 1)) * h
    x = page[:, unstriped(offs3)] + f64(b)[:, None]
    w2 = unpack_weight(w2_words, w2_scales, "e2m1")
    cells = w2.T @ mxq(x, 0, "e4m3")
    days = mxq(f64(w3), 0, "e4m3").T @ mxq(h, 0, "e4m3")
    y = np.maximum(cells, days)
    words, scales = planes(page)
    return y, page, words, scales

@@ -1,0 +1,344 @@
+from contextlib import ExitStack
+
+import concourse.mybir as mybir
+
+K, T, S, H, T2, N = 1536, 2048, 1024, 1024, 2048, 512
+FLOPS = 2 * K * H * S + 2 * 2 * H * N * S
+
+F32 = mybir.dt.float32
+BF16 = mybir.dt.bfloat16
+I32 = mybir.dt.int32
+U32 = mybir.dt.uint32
+U16 = mybir.dt.uint16
+U8 = mybir.dt.uint8
+FP8X4 = mybir.dt.float8_e4m3fn_x4
+FP4X4 = mybir.dt.float4_e2m1fn_x4
+ALU = mybir.AluOpType
+COPY = mybir.ActivationFunctionType.Copy
+
+P = 128
+PACK = 4
+PASS = P * PACK
+BANK = 512
+K_PASSES = K // PASS
+GROUPS = H // PASS
+HALVES = S // BANK
+QUADS = 4
+PAGE_SLOTS = 4
+
+
+def tile_list_pasture_board_scores_kernel(
+    tc, tab_words, tab_scales, offs, w1, al, page0, wgs, offs2, offs3, b, w2_words, w2_scales, w3, out_0, out_1, out_2, out_3
+):
+    nc = tc.nc
+    with ExitStack() as ctx:
+        sb = ctx.enter_context(tc.tile_pool(name="sb", bufs=1))
+        psum = ctx.enter_context(tc.psum_pool(name="psum", bufs=1))
+
+        def sbuf(shape, dtype, tag):
+            return sb.tile(shape, dtype, name=tag, tag=tag, align_bytes=64)
+
+        def cols(i, width=BANK):
+            return slice(i * width, (i + 1) * width)
+
+        banks = [psum.tile([P, BANK], F32, name="bank%d" % i) for i in range(8)]
+        page_rows = page0.rearrange("(g p t) c -> g t p c", p=P, t=PACK)
+        out_rows = out_1.rearrange("(g p t) c -> g t p c", p=P, t=PACK)
+        wgs_rows = wgs.rearrange("(q t) j -> q t j", t=PACK)
+
+        def load_weight(w, a, g, slot):
+            raw = sbuf([P, PACK, BANK], F32, "big%d" % slot)
+            nc.sync.dma_start(out=raw[:], in_=w[cols(a, PASS), cols(g)].rearrange("(p j) c -> p j c", j=PACK))
+            return raw
+
+        def load_table(a):
+            words = sbuf([P, T], U32, "tab_words%d" % a)
+            nc.sync.dma_start(out=words[:].bitcast(I32), in_=tab_words[a].rearrange("p c i -> p (c i)").bitcast(I32))
+            return words
+
+        def load_list(src, name):
+            lst = sbuf([P, S // 16], U16, name)
+            nc.sync.dma_start(lst[:], src)
+            return lst
+
+        def load_page(g, t):
+            page = sbuf([P, T2], F32, "page%d" % ((PACK * g + t) % PAGE_SLOTS))
+            nc.sync.dma_start(out=page[:], in_=page_rows[g, t])
+            return page
+
+        rounded_count = []
+
+        def rounded_tile():
+            rounded_count.append(1)
+            return sbuf([P, PACK * BANK], BF16, "rounded%d" % (len(rounded_count) % 4))
+
+        def interleave(engine_copy, src, dst=None):
+            if dst is None:
+                dst = rounded_tile()[:]
+            engine_copy(
+                out=dst.rearrange("p (c i t) -> p c t i", i=4, t=PACK),
+                in_=src.rearrange("p t (c i) -> p c t i", i=4),
+            )
+            return dst
+
+        def quantise(rounded, slot):
+            codes = sbuf([P, BANK], U32, "codes%d" % slot)
+            scales = sbuf([P, BANK], U8, "scales%d" % slot)
+            nc.vector.quantize_mx(out=codes[:].bitcast(FP8X4), scales=scales[:], in_=rounded)
+            return codes, scales
+
+        tab_sc = sbuf([P, T], U8, "tab_scales")
+        w2_sc = sbuf([P, GROUPS, N], U8, "w2_scales")
+        nc.gpsimd.memset(tab_sc[:].bitcast(I32), 0)
+        nc.gpsimd.memset(w2_sc[:].bitcast(I32), 0)
+
+        w1_raw = {}
+        tab = {}
+        w1_raw[0, 0] = load_weight(w1, 0, 0, 0)
+        tab[0] = load_table(0)
+        list1 = load_list(offs, "list1")
+        b_sb = sbuf([P, GROUPS, PACK], F32, "b")
+        nc.scalar.dma_start(out=b_sb[:], in_=b.rearrange("(g p t) -> p g t", p=P, t=PACK))
+        for q in range(QUADS):
+            nc.scalar.dma_start(
+                out=tab_sc[32 * q : 32 * q + 4 * K_PASSES, :].bitcast(I32),
+                in_=tab_scales[:, 4 * q : 4 * q + 4, :].bitcast(I32),
+            )
+        al_sb = sbuf([P, GROUPS, PACK], F32, "al")
+        nc.scalar.dma_start(out=al_sb[:], in_=al.rearrange("(g p t) -> p g t", p=P, t=PACK))
+        for a in range(1, K_PASSES):
+            w1_raw[a, 0] = load_weight(w1, a, 0, a)
+            tab[a] = load_table(a)
+        list2 = load_list(offs2, "list2")
+        wg_first = sbuf([P, S], F32, "wg_first")
+        wg_rest = sbuf([P, PACK - 1, S], F32, "wg_rest")
+        for q in range(QUADS):
+            nc.sync.dma_start(out=wg_first[32 * q : 32 * q + 32, :], in_=wgs_rows[:, 0, :])
+        pages = {}
+        pages[0, 0] = load_page(0, 0)
+        list3 = load_list(offs3, "list3")
+
+        bias = {}
+
+        def spread_bias(engine_copy, g, t0, count, tag):
+            spread = sbuf([P, count, BANK], F32, tag)
+            engine_copy(out=spread[:], in_=b_sb[:, g, t0 : t0 + count].unsqueeze(2).to_broadcast([P, count, BANK]))
+            for i in range(count):
+                bias[g, t0 + i] = spread[:, i, :]
+
+        spread_bias(nc.vector.tensor_copy, 0, 0, PACK, "bias")
+
+        picked = [sbuf([P, S], U32, "picked%d" % a) for a in range(K_PASSES)]
+        picked_sc = sbuf([P, S], U8, "picked_scales")
+
+        def first_stage_pass(a, g):
+            rounded = rounded_tile()
+            nc.scalar.copy(
+                out=rounded[:].rearrange("p (t m j) -> p m j t", t=PACK, j=PACK),
+                in_=w1_raw[a, g][:].rearrange("p j (m t) -> p m j t", t=PACK),
+            )
+            codes, scales = quantise(rounded[:], K_PASSES * g + a)
+            for t in range(PACK):
+                for half in range(HALVES):
+                    nc.tensor.matmul_mx(
+                        out=banks[HALVES * t + half][:],
+                        lhsT=codes[:, cols(t, P)].bitcast(FP8X4),
+                        lhsT_scale=scales[:, cols(t, P)],
+                        rhs=picked[a][:, cols(half)].bitcast(FP8X4),
+                        rhs_scale=picked_sc[4 * a : P, cols(half)],
+                        start=(a == 0),
+                        stop=(a == K_PASSES - 1),
+                    )
+
+        h = {}
+
+        def features(g, t):
+            for half in range(HALVES):
+                bank = banks[HALVES * t + half]
+                feat = h[g][:, t, cols(half)]
+                nc.scalar.activation(out=feat, in_=bank[:], func=COPY, scale=al_sb[:, g, t : t + 1])
+                nc.vector.tensor_tensor(out=feat, in0=bank[:], in1=feat, op=ALU.max)
+
+        def renew(g, t):
+            weight = wg_first[:] if t == 0 else wg_rest[:, t - 1, :]
+            nc.vector.tensor_tensor(out=pages[g, t][:].indirect(list2[:]), in0=h[g][:, t, :], in1=weight, op=ALU.mult)
+
+        x = {}
+        stage = {}
+
+        def read_cells(g, t):
+            for half in range(HALVES):
+                nc.vector.tensor_tensor(
+                    out=x[g][:, t, cols(half)],
+                    in0=pages[g, t][:].indirect(list3[:, cols(half, BANK // 16)]),
+                    in1=bias[g, t],
+                    op=ALU.add,
+                )
+
+        def round_page(g, t, sides=(0, 1)):
+            if 0 in sides:
+                queue = nc.sync if (g, t) == (GROUPS - 1, PACK - 1) else nc.scalar
+                queue.dma_start(out=out_rows[g, t], in_=pages[g, t][:])
+            for side in sides:
+                nc.scalar.copy(out=stage[g][side][:, t, :], in_=pages[g, t][:, cols(side, T2 // 2)])
+
+        plane_sc = sbuf([P, GROUPS, T2], U8, "plane_scales")
+        plane_words = [sbuf([P, T2], U32, "plane_words%d" % g) for g in range(GROUPS)]
+
+        def planes_chunk(g, c, engine_copy, dst=None):
+            rounded = interleave(engine_copy, stage[g][c // 2][:, :, cols(c % 2)], dst)
+            nc.vector.quantize_mx(out=plane_words[g][:, cols(c)].bitcast(FP8X4), scales=plane_sc[:, g, cols(c)], in_=rounded)
+
+        def store_plane_words(g, first, count):
+            span = slice(first * BANK, (first + count) * BANK)
+            nc.sync.dma_start(
+                out=out_2[g].rearrange("p m t -> p (m t)").bitcast(I32)[:, span], in_=plane_words[g][:, span].bitcast(I32)
+            )
+
+        def store_plane_scales():
+            for q in range(QUADS):
+                nc.sync.dma_start(
+                    out=out_3[:, 4 * q : 4 * q + 4, :].rearrange("g r c -> r g c").bitcast(I32),
+                    in_=plane_sc[32 * q : 32 * q + 4, :, :].bitcast(I32),
+                )
+
+        nc.vector.tensor_copy(out=picked[0][:], in_=tab[0][:].indirect(list1[:]))
+        nc.vector.tensor_copy(out=picked_sc[:], in_=tab_sc[:].indirect(list1[:]))
+        first_stage_pass(0, 0)
+        nc.vector.tensor_copy(out=picked[1][:], in_=tab[1][:].indirect(list1[:]))
+        first_stage_pass(1, 0)
+        for half in range(HALVES):
+            nc.vector.tensor_copy(out=picked[2][:, cols(half)], in_=tab[2][:].indirect(list1[:, cols(half, BANK // 16)]))
+        first_stage_pass(2, 0)
+
+        w1_raw[0, 1] = load_weight(w1, 0, 1, 3)
+        w1_raw[1, 1] = load_weight(w1, 1, 1, 0)
+        w1_raw[2, 1] = load_weight(w1, 2, 1, 1)
+        for q in range(QUADS):
+            nc.sync.dma_start(out=wg_rest[32 * q : 32 * q + 32, :, :], in_=wgs_rows[:, 1:PACK, :])
+        pages[0, 1] = load_page(0, 1)
+
+        h[0] = sbuf([P, PACK, S], F32, "act0")
+        features(0, 0)
+        renew(0, 0)
+        for t in range(1, PACK):
+            features(0, t)
+        for a in range(K_PASSES):
+            first_stage_pass(a, 1)
+
+        w3_raw = [load_weight(w3, a, 0, a) for a in range(GROUPS)]
+        pages[0, 2] = load_page(0, 2)
+        pages[0, 3] = load_page(0, 3)
+        w2_w = sbuf([P, GROUPS, 2 * N], U8, "w2_words")
+        nc.sync.dma_start(out=w2_w[:].bitcast(I32), in_=w2_words.rearrange("a p c -> p a c").bitcast(I32))
+        for q in range(QUADS):
+            nc.sync.dma_start(
+                out=w2_sc[32 * q : 32 * q + 4, :, :].bitcast(I32),
+                in_=w2_scales[:, 4 * q : 4 * q + 4, :].rearrange("a r c -> r a c").bitcast(I32),
+            )
+
+        def days_scores(h_q, w3_q):
+            for n in range(N // P):
+                for half in range(HALVES):
+                    bank = banks[HALVES * n + half]
+                    for g in range(GROUPS):
+                        nc.tensor.matmul_mx(
+                            out=bank[:],
+                            lhsT=w3_q[g][0][:, cols(n, P)].bitcast(FP8X4),
+                            lhsT_scale=w3_q[g][1][:, cols(n, P)],
+                            rhs=h_q[g, half][0][:].bitcast(FP8X4),
+                            rhs_scale=h_q[g, half][1][:],
+                            start=(g == 0),
+                            stop=(g == GROUPS - 1),
+                        )
+                    nc.scalar.copy(out=days[n // 2][:, n % 2, cols(half)], in_=bank[:])
+
+        def cells_pass(g, half, codes, scales):
+            for n in range(N // P):
+                nc.tensor.matmul_mx(
+                    out=banks[HALVES * n + half][:],
+                    lhsT=w2_w[:, g, cols(n, 2 * P)].bitcast(FP4X4),
+                    lhsT_scale=w2_sc[:, g, cols(n, P)],
+                    rhs=codes[:].bitcast(FP8X4),
+                    rhs_scale=scales[:],
+                    start=(g == 0),
+                    stop=(g == GROUPS - 1),
+                )
+
+        def scores(half):
+            for n in range(N // P):
+                best = days[n // 2][:, n % 2, cols(half)]
+                nc.vector.tensor_tensor(out=best, in0=banks[HALVES * n + half][:], in1=best, op=ALU.max)
+                nc.sync.dma_start(out=out_0[cols(n, P), cols(half)], in_=best)
+
+        x[0] = sbuf([P, PACK, S], F32, "act2")
+        stage[0] = [sbuf([P, PACK, T2 // 2], BF16, "big%d" % (2 + side)) for side in range(2)]
+        h_q = {}
+        read_cells(0, 0)
+        round_page(0, 0)
+        pages[1, 0] = load_page(1, 0)
+        for half in range(HALVES):
+            h_q[0, half] = quantise(interleave(nc.scalar.copy, h[0][:, :, cols(half)]), half)
+        renew(0, 1)
+
+        h[1] = sbuf([P, PACK, S], F32, "act1")
+        for t in range(PACK):
+            features(1, t)
+        read_cells(0, 1)
+        w3_q = [quantise(interleave(nc.scalar.copy, w3_raw[a][:]), 6 + a) for a in range(GROUPS)]
+        round_page(0, 1)
+        pages[1, 1] = load_page(1, 1)
+        renew(0, 2)
+        read_cells(0, 2)
+
+        for half in range(HALVES):
+            h_q[1, half] = quantise(interleave(nc.scalar.copy, h[1][:, :, cols(half)]), 3 + half)
+        for i in range(2):
+            spread_bias(nc.scalar.copy, 1, 2 * i, 2, "picked%d" % i)
+        round_page(0, 2)
+        pages[1, 2] = load_page(1, 2)
+        renew(0, 3)
+        read_cells(0, 3)
+        round_page(0, 3)
+        pages[1, 3] = load_page(1, 3)
+        renew(1, 0)
+
+        held = [sbuf([P, 2, PACK * BANK], BF16, "tab_words%d" % a) for a in range(K_PASSES)]
+        for c in range(T2 // BANK):
+            planes_chunk(0, c, nc.scalar.copy, held[c // 2][:, c % 2, :])
+        store_plane_words(0, 0, T2 // BANK)
+
+        x[1] = sbuf([P, PACK, S], F32, "act0")
+        stage[1] = [sbuf([P, PACK, T2 // 2], BF16, "big%d" % (2 + side)) for side in range(2)]
+        read_cells(1, 0)
+        round_page(1, 0)
+        renew(1, 1)
+        x_q = [
+            quantise(interleave(nc.scalar.copy, x[0][:, :, cols(half)], held[2][:, half, :]), 2 + 3 * half)
+            for half in range(HALVES)
+        ]
+        read_cells(1, 1)
+        round_page(1, 1)
+        renew(1, 2)
+        days = [sbuf([P, 2, S], F32, "big%d" % nn) for nn in range(2)]
+        days_scores(h_q, w3_q)
+        for half in range(HALVES):
+            cells_pass(0, half, *x_q[half])
+        read_cells(1, 2)
+        round_page(1, 2)
+        renew(1, 3)
+        read_cells(1, 3)
+
+        round_page(1, 3, (0,))
+        cells_pass(1, 0, *quantise(interleave(nc.scalar.copy, x[1][:, :, cols(0)]), 0))
+        round_page(1, 3, (1,))
+        cells_pass(1, 1, *quantise(interleave(nc.scalar.copy, x[1][:, :, cols(1)]), 1))
+        planes_chunk(1, 0, nc.vector.tensor_copy)
+        planes_chunk(1, 1, nc.vector.tensor_copy)
+        store_plane_words(1, 0, 2)
+        planes_chunk(1, 2, nc.scalar.copy)
+        scores(0)
+        planes_chunk(1, 3, nc.scalar.copy)
+        store_plane_words(1, 2, 2)
+        store_plane_scales()
+        scores(1)

@@ -15,6 +15,7 @@ FP8X4 = mybir.dt.float8_e4m3fn_x4
 FP4X4 = mybir.dt.float4_e2m1fn_x4
 ALU = mybir.AluOpType
 COPY = mybir.ActivationFunctionType.Copy
+IDENTITY = mybir.ActivationFunctionType.Identity
 
 P = 128
 PACK = 4
@@ -24,7 +25,7 @@ K_PASSES = K // PASS
 GROUPS = H // PASS
 HALVES = S // BANK
 QUADS = 4
-PAGE_SLOTS = 4
+QUAD_ORDER = (0, 2, 1, 3)
 
 
 def tile_list_pasture_board_scores_kernel(
@@ -46,9 +47,8 @@ def tile_list_pasture_board_scores_kernel(
         out_rows = out_1.rearrange("(g p t) c -> g t p c", p=P, t=PACK)
         wgs_rows = wgs.rearrange("(q t) j -> q t j", t=PACK)
 
-        def load_weight(w, a, g, slot):
-            raw = sbuf([P, PACK, BANK], F32, "big%d" % slot)
-            nc.sync.dma_start(out=raw[:], in_=w[cols(a, PASS), cols(g)].rearrange("(p j) c -> p j c", j=PACK))
+        def load_weight(w, a, g, raw):
+            nc.sync.dma_start(out=raw, in_=w[cols(a, PASS), cols(g)].rearrange("(p j) c -> p j c", j=PACK))
             return raw
 
         def load_table(a):
@@ -61,8 +61,8 @@ def tile_list_pasture_board_scores_kernel(
             nc.sync.dma_start(lst[:], src)
             return lst
 
-        def load_page(g, t):
-            page = sbuf([P, T2], F32, "page%d" % ((PACK * g + t) % PAGE_SLOTS))
+        def load_page(g, t, slot):
+            page = sbuf([P, T2], F32, "big%d" % slot)
             nc.sync.dma_start(out=page[:], in_=page_rows[g, t])
             return page
 
@@ -70,7 +70,7 @@ def tile_list_pasture_board_scores_kernel(
 
         def rounded_tile():
             rounded_count.append(1)
-            return sbuf([P, PACK * BANK], BF16, "rounded%d" % (len(rounded_count) % 4))
+            return sbuf([P, PACK * BANK], BF16, "rounded%d" % (len(rounded_count) % 5))
 
         def interleave(engine_copy, src, dst=None):
             if dst is None:
@@ -89,66 +89,68 @@ def tile_list_pasture_board_scores_kernel(
 
         tab_sc = sbuf([P, T], U8, "tab_scales")
         w2_sc = sbuf([P, GROUPS, N], U8, "w2_scales")
-        nc.gpsimd.memset(tab_sc[:].bitcast(I32), 0)
-        nc.gpsimd.memset(w2_sc[:].bitcast(I32), 0)
+        nc.vector.memset(tab_sc[:].bitcast(I32), 0)
+        nc.vector.memset(w2_sc[:].bitcast(I32), 0)
 
         w1_raw = {}
+        w1_group0 = sbuf([P, K_PASSES, PACK, BANK], F32, "wide")
         tab = {}
-        w1_raw[0, 0] = load_weight(w1, 0, 0, 0)
+        w1_raw[0, 0] = load_weight(w1, 0, 0, w1_group0[:, 0, :, :])
         tab[0] = load_table(0)
         list1 = load_list(offs, "list1")
-        b_sb = sbuf([P, GROUPS, PACK], F32, "b")
-        nc.scalar.dma_start(out=b_sb[:], in_=b.rearrange("(g p t) -> p g t", p=P, t=PACK))
         for q in range(QUADS):
             nc.scalar.dma_start(
                 out=tab_sc[32 * q : 32 * q + 4 * K_PASSES, :].bitcast(I32),
                 in_=tab_scales[:, 4 * q : 4 * q + 4, :].bitcast(I32),
             )
+        w1_raw[1, 0] = load_weight(w1, 1, 0, w1_group0[:, 1, :, :])
+        tab[1] = load_table(1)
+        w1_raw[2, 0] = load_weight(w1, 2, 0, w1_group0[:, 2, :, :])
         al_sb = sbuf([P, GROUPS, PACK], F32, "al")
-        nc.scalar.dma_start(out=al_sb[:], in_=al.rearrange("(g p t) -> p g t", p=P, t=PACK))
-        for a in range(1, K_PASSES):
-            w1_raw[a, 0] = load_weight(w1, a, 0, a)
-            tab[a] = load_table(a)
+        nc.sync.dma_start(out=al_sb[:], in_=al.rearrange("(g p t) -> p g t", p=P, t=PACK))
+        tab[2] = load_table(2)
         list2 = load_list(offs2, "list2")
-        wg_first = sbuf([P, S], F32, "wg_first")
-        wg_rest = sbuf([P, PACK - 1, S], F32, "wg_rest")
-        for q in range(QUADS):
-            nc.sync.dma_start(out=wg_first[32 * q : 32 * q + 32, :], in_=wgs_rows[:, 0, :])
-        pages = {}
-        pages[0, 0] = load_page(0, 0)
-        list3 = load_list(offs3, "list3")
+        weights = {}
 
-        bias = {}
-
-        def spread_bias(engine_copy, g, t0, count, tag):
-            spread = sbuf([P, count, BANK], F32, tag)
-            engine_copy(out=spread[:], in_=b_sb[:, g, t0 : t0 + count].unsqueeze(2).to_broadcast([P, count, BANK]))
+        def load_wgs(t0, count):
+            dealt = sbuf([P, count, S], F32, "wgs%d" % t0)
+            for q in QUAD_ORDER:
+                nc.sync.dma_start(out=dealt[32 * q : 32 * q + 32, :, :], in_=wgs_rows[:, t0 : t0 + count, :])
             for i in range(count):
-                bias[g, t0 + i] = spread[:, i, :]
+                weights[t0 + i] = dealt[:, i, :]
 
-        spread_bias(nc.vector.tensor_copy, 0, 0, PACK, "bias")
+        load_wgs(0, 1)
+        pages = {}
+        pages[0, 0] = load_page(0, 0, 3)
+        list3 = load_list(offs3, "list3")
+        b_sb = sbuf([P, GROUPS, PACK], F32, "b")
+        nc.sync.dma_start(out=b_sb[:], in_=b.rearrange("(g p t) -> p g t", p=P, t=PACK))
 
         picked = [sbuf([P, S], U32, "picked%d" % a) for a in range(K_PASSES)]
         picked_sc = sbuf([P, S], U8, "picked_scales")
 
-        def first_stage_pass(a, g):
+        def quantise_w1(a, g):
             rounded = rounded_tile()
             nc.scalar.copy(
                 out=rounded[:].rearrange("p (t m j) -> p m j t", t=PACK, j=PACK),
-                in_=w1_raw[a, g][:].rearrange("p j (m t) -> p m j t", t=PACK),
+                in_=w1_raw[a, g].rearrange("p j (m t) -> p m j t", t=PACK),
             )
-            codes, scales = quantise(rounded[:], K_PASSES * g + a)
+            return quantise(rounded[:], K_PASSES * g + a)
+
+        def first_stage(w1_q):
             for t in range(PACK):
                 for half in range(HALVES):
-                    nc.tensor.matmul_mx(
-                        out=banks[HALVES * t + half][:],
-                        lhsT=codes[:, cols(t, P)].bitcast(FP8X4),
-                        lhsT_scale=scales[:, cols(t, P)],
-                        rhs=picked[a][:, cols(half)].bitcast(FP8X4),
-                        rhs_scale=picked_sc[4 * a : P, cols(half)],
-                        start=(a == 0),
-                        stop=(a == K_PASSES - 1),
-                    )
+                    for a in range(K_PASSES):
+                        codes, scales = w1_q[a]
+                        nc.tensor.matmul_mx(
+                            out=banks[HALVES * t + half][:],
+                            lhsT=codes[:, cols(t, P)].bitcast(FP8X4),
+                            lhsT_scale=scales[:, cols(t, P)],
+                            rhs=picked[a][:, cols(half)].bitcast(FP8X4),
+                            rhs_scale=picked_sc[4 * a : P, cols(half)],
+                            start=(a == 0),
+                            stop=(a == K_PASSES - 1),
+                        )
 
         h = {}
 
@@ -160,25 +162,26 @@ def tile_list_pasture_board_scores_kernel(
                 nc.vector.tensor_tensor(out=feat, in0=bank[:], in1=feat, op=ALU.max)
 
         def renew(g, t):
-            weight = wg_first[:] if t == 0 else wg_rest[:, t - 1, :]
-            nc.vector.tensor_tensor(out=pages[g, t][:].indirect(list2[:]), in0=h[g][:, t, :], in1=weight, op=ALU.mult)
+            nc.vector.tensor_tensor(out=pages[g, t][:].indirect(list2[:]), in0=h[g][:, t, :], in1=weights[t], op=ALU.mult)
 
         x = {}
+
+        def read_cells(g, t, pieces=1):
+            cells = sbuf([P, S], F32, ("cells", "picked0")[t % 2])
+            width = S // pieces
+            for i in range(pieces):
+                nc.vector.tensor_copy(out=cells[:, cols(i, width)], in_=pages[g, t][:].indirect(list3[:, cols(i, width // 16)]))
+            return cells
+
+        def add_bias(g, t, cells, span=slice(0, S)):
+            nc.scalar.activation(out=x[g][:, t, span], in_=cells[:, span], func=IDENTITY, bias=b_sb[:, g, t : t + 1])
+
+        def store_page(queue, g, t):
+            queue.dma_start(out=out_rows[g, t], in_=pages[g, t][:])
+
         stage = {}
 
-        def read_cells(g, t):
-            for half in range(HALVES):
-                nc.vector.tensor_tensor(
-                    out=x[g][:, t, cols(half)],
-                    in0=pages[g, t][:].indirect(list3[:, cols(half, BANK // 16)]),
-                    in1=bias[g, t],
-                    op=ALU.add,
-                )
-
         def round_page(g, t, sides=(0, 1)):
-            if 0 in sides:
-                queue = nc.sync if (g, t) == (GROUPS - 1, PACK - 1) else nc.scalar
-                queue.dma_start(out=out_rows[g, t], in_=pages[g, t][:])
             for side in sides:
                 nc.scalar.copy(out=stage[g][side][:, t, :], in_=pages[g, t][:, cols(side, T2 // 2)])
 
@@ -204,31 +207,22 @@ def tile_list_pasture_board_scores_kernel(
 
         nc.vector.tensor_copy(out=picked[0][:], in_=tab[0][:].indirect(list1[:]))
         nc.vector.tensor_copy(out=picked_sc[:], in_=tab_sc[:].indirect(list1[:]))
-        first_stage_pass(0, 0)
+        w1_q = [quantise_w1(0, 0)]
         nc.vector.tensor_copy(out=picked[1][:], in_=tab[1][:].indirect(list1[:]))
-        first_stage_pass(1, 0)
+        w1_q.append(quantise_w1(1, 0))
+        w1_q.append(quantise_w1(2, 0))
         for half in range(HALVES):
             nc.vector.tensor_copy(out=picked[2][:, cols(half)], in_=tab[2][:].indirect(list1[:, cols(half, BANK // 16)]))
-        first_stage_pass(2, 0)
+        first_stage(w1_q)
 
-        w1_raw[0, 1] = load_weight(w1, 0, 1, 3)
-        w1_raw[1, 1] = load_weight(w1, 1, 1, 0)
-        w1_raw[2, 1] = load_weight(w1, 2, 1, 1)
-        for q in range(QUADS):
-            nc.sync.dma_start(out=wg_rest[32 * q : 32 * q + 32, :, :], in_=wgs_rows[:, 1:PACK, :])
-        pages[0, 1] = load_page(0, 1)
-
-        h[0] = sbuf([P, PACK, S], F32, "act0")
-        features(0, 0)
-        renew(0, 0)
-        for t in range(1, PACK):
-            features(0, t)
-        for a in range(K_PASSES):
-            first_stage_pass(a, 1)
-
-        w3_raw = [load_weight(w3, a, 0, a) for a in range(GROUPS)]
-        pages[0, 2] = load_page(0, 2)
-        pages[0, 3] = load_page(0, 3)
+        w1_group1 = sbuf([P, K_PASSES, PACK, BANK], F32, "wide")
+        w1_raw[0, 1] = load_weight(w1, 0, 1, w1_group1[:, 0, :, :])
+        w1_raw[1, 1] = load_weight(w1, 1, 1, w1_group1[:, 1, :, :])
+        load_wgs(1, 1)
+        w1_raw[2, 1] = load_weight(w1, 2, 1, w1_group1[:, 2, :, :])
+        pages[0, 1] = load_page(0, 1, 5)
+        load_wgs(2, 2)
+        w3_raw = [load_weight(w3, a, 0, sbuf([P, PACK, BANK], F32, "big%d" % (2, 6)[a])[:]) for a in range(GROUPS)]
         w2_w = sbuf([P, GROUPS, 2 * N], U8, "w2_words")
         nc.sync.dma_start(out=w2_w[:].bitcast(I32), in_=w2_words.rearrange("a p c -> p a c").bitcast(I32))
         for q in range(QUADS):
@@ -236,6 +230,15 @@ def tile_list_pasture_board_scores_kernel(
                 out=w2_sc[32 * q : 32 * q + 4, :, :].bitcast(I32),
                 in_=w2_scales[:, 4 * q : 4 * q + 4, :].rearrange("a r c -> r a c").bitcast(I32),
             )
+
+        h[0] = sbuf([P, PACK, S], F32, "act0")
+        features(0, 0)
+        renew(0, 0)
+        for t in range(1, PACK):
+            features(0, t)
+        first_stage([quantise_w1(a, 1) for a in range(K_PASSES)])
+        pages[0, 2] = load_page(0, 2, 7)
+        pages[0, 3] = load_page(0, 3, 8)
 
         def days_scores(h_q, w3_q):
             for n in range(N // P):
@@ -271,74 +274,75 @@ def tile_list_pasture_board_scores_kernel(
                 nc.vector.tensor_tensor(out=best, in0=banks[HALVES * n + half][:], in1=best, op=ALU.max)
                 nc.sync.dma_start(out=out_0[cols(n, P), cols(half)], in_=best)
 
-        x[0] = sbuf([P, PACK, S], F32, "act2")
-        stage[0] = [sbuf([P, PACK, T2 // 2], BF16, "big%d" % (2 + side)) for side in range(2)]
-        h_q = {}
-        read_cells(0, 0)
-        round_page(0, 0)
-        pages[1, 0] = load_page(1, 0)
-        for half in range(HALVES):
-            h_q[0, half] = quantise(interleave(nc.scalar.copy, h[0][:, :, cols(half)]), half)
-        renew(0, 1)
+        def finish_page(g, t):
+            cells = read_cells(g, t)
+            store_page(nc.scalar, g, t)
+            round_page(g, t)
+            add_bias(g, t, cells)
 
+        wide = sbuf([P, 4, PACK, S], BF16, "wide")
+        x[0] = wide[:, 0, :, :]
+        stage[0] = [wide[:, 1 + side, :, :] for side in range(2)]
+        h_rounded = wide[:, 3, :, :].rearrange("p (half a) c -> p half (a c)", half=HALVES)
+        h_q = {}
         h[1] = sbuf([P, PACK, S], F32, "act1")
+        renew(0, 1)
+        finish_page(0, 0)
+        for half in range(HALVES):
+            h_q[0, half] = quantise(interleave(nc.scalar.copy, h[0][:, :, cols(half)], h_rounded[:, half, :]), half)
         for t in range(PACK):
             features(1, t)
-        read_cells(0, 1)
-        w3_q = [quantise(interleave(nc.scalar.copy, w3_raw[a][:]), 6 + a) for a in range(GROUPS)]
-        round_page(0, 1)
-        pages[1, 1] = load_page(1, 1)
         renew(0, 2)
-        read_cells(0, 2)
-
+        finish_page(0, 1)
+        w3_q = [quantise(interleave(nc.scalar.copy, w3_raw[a]), 6 + a) for a in range(GROUPS)]
+        pages[1, 0] = load_page(1, 0, 2)
+        pages[1, 1] = load_page(1, 1, 6)
         for half in range(HALVES):
             h_q[1, half] = quantise(interleave(nc.scalar.copy, h[1][:, :, cols(half)]), 3 + half)
-        for i in range(2):
-            spread_bias(nc.scalar.copy, 1, 2 * i, 2, "picked%d" % i)
-        round_page(0, 2)
-        pages[1, 2] = load_page(1, 2)
+        finish_page(0, 2)
+        pages[1, 2] = load_page(1, 2, 7)
         renew(0, 3)
-        read_cells(0, 3)
-        round_page(0, 3)
-        pages[1, 3] = load_page(1, 3)
+        finish_page(0, 3)
         renew(1, 0)
 
-        held = [sbuf([P, 2, PACK * BANK], BF16, "tab_words%d" % a) for a in range(K_PASSES)]
-        for c in range(T2 // BANK):
-            planes_chunk(0, c, nc.scalar.copy, held[c // 2][:, c % 2, :])
-        store_plane_words(0, 0, T2 // BANK)
-
-        x[1] = sbuf([P, PACK, S], F32, "act0")
-        stage[1] = [sbuf([P, PACK, T2 // 2], BF16, "big%d" % (2 + side)) for side in range(2)]
-        read_cells(1, 0)
-        round_page(1, 0)
-        renew(1, 1)
+        held = [sbuf([P, 2, PACK * BANK], BF16, "tab_words%d" % a) for a in range(2)]
         x_q = [
-            quantise(interleave(nc.scalar.copy, x[0][:, :, cols(half)], held[2][:, half, :]), 2 + 3 * half)
+            quantise(interleave(nc.scalar.copy, x[0][:, :, cols(half)]), 2 + 3 * half)
             for half in range(HALVES)
         ]
-        read_cells(1, 1)
-        round_page(1, 1)
-        renew(1, 2)
-        days = [sbuf([P, 2, S], F32, "big%d" % nn) for nn in range(2)]
+        days = [sbuf([P, 2, S], F32, ("big3", "tab_words2")[nn]) for nn in range(2)]
         days_scores(h_q, w3_q)
         for half in range(HALVES):
             cells_pass(0, half, *x_q[half])
-        read_cells(1, 2)
-        round_page(1, 2)
+
+        x[1] = sbuf([P, PACK, S], BF16, "act0")
+        stage[1] = [sbuf([P, PACK, T2 // 2], BF16, "big%d" % (5, 8)[side]) for side in range(2)]
+        finish_page(1, 0)
+        pages[1, 3] = load_page(1, 3, 2)
+        renew(1, 1)
+        for c in range(T2 // BANK):
+            planes_chunk(0, c, nc.scalar.copy, held[c // 2][:, c % 2, :])
+        store_plane_words(0, 0, T2 // BANK)
+        finish_page(1, 1)
+        renew(1, 2)
+        finish_page(1, 2)
         renew(1, 3)
-        read_cells(1, 3)
+        store_page(nc.sync, 1, 3)
+        cells = read_cells(1, 3, HALVES)
 
         round_page(1, 3, (0,))
+        add_bias(1, 3, cells, cols(0))
         cells_pass(1, 0, *quantise(interleave(nc.scalar.copy, x[1][:, :, cols(0)]), 0))
-        round_page(1, 3, (1,))
+        add_bias(1, 3, cells, cols(1))
         cells_pass(1, 1, *quantise(interleave(nc.scalar.copy, x[1][:, :, cols(1)]), 1))
+        round_page(1, 3, (1,))
         planes_chunk(1, 0, nc.vector.tensor_copy)
         planes_chunk(1, 1, nc.vector.tensor_copy)
         store_plane_words(1, 0, 2)
         planes_chunk(1, 2, nc.scalar.copy)
+        store_plane_words(1, 2, 1)
         scores(0)
         planes_chunk(1, 3, nc.scalar.copy)
-        store_plane_words(1, 2, 2)
+        store_plane_words(1, 3, 1)
         store_plane_scales()
         scores(1)

from contextlib import ExitStack

import concourse.mybir as mybir

K, T, S, H, T2, N = 1536, 2048, 1024, 1024, 2048, 512
FLOPS = 2 * K * H * S + 2 * 2 * H * N * S

F32 = mybir.dt.float32
BF16 = mybir.dt.bfloat16
I32 = mybir.dt.int32
U32 = mybir.dt.uint32
U16 = mybir.dt.uint16
U8 = mybir.dt.uint8
FP8X4 = mybir.dt.float8_e4m3fn_x4
FP4X4 = mybir.dt.float4_e2m1fn_x4
ALU = mybir.AluOpType
COPY = mybir.ActivationFunctionType.Copy
IDENTITY = mybir.ActivationFunctionType.Identity

P = 128
PACK = 4
PASS = P * PACK
BANK = 512
K_PASSES = K // PASS
GROUPS = H // PASS
HALVES = S // BANK
QUADS = 4
QUAD_ORDER = (0, 2, 1, 3)


def tile_list_pasture_board_scores_kernel(
    tc, tab_words, tab_scales, offs, w1, al, page0, wgs, offs2, offs3, b, w2_words, w2_scales, w3, out_0, out_1, out_2, out_3
):
    nc = tc.nc
    with ExitStack() as ctx:
        sb = ctx.enter_context(tc.tile_pool(name="sb", bufs=1))
        psum = ctx.enter_context(tc.psum_pool(name="psum", bufs=1))

        def sbuf(shape, dtype, tag):
            return sb.tile(shape, dtype, name=tag, tag=tag, align_bytes=64)

        def cols(i, width=BANK):
            return slice(i * width, (i + 1) * width)

        banks = [psum.tile([P, BANK], F32, name="bank%d" % i) for i in range(8)]
        page_rows = page0.rearrange("(g p t) c -> g t p c", p=P, t=PACK)
        out_rows = out_1.rearrange("(g p t) c -> g t p c", p=P, t=PACK)
        wgs_rows = wgs.rearrange("(q t) j -> q t j", t=PACK)

        def load_weight(w, a, g, raw):
            nc.sync.dma_start(out=raw, in_=w[cols(a, PASS), cols(g)].rearrange("(p j) c -> p j c", j=PACK))
            return raw

        def load_table(a):
            words = sbuf([P, T], U32, "tab_words%d" % a)
            nc.sync.dma_start(out=words[:].bitcast(I32), in_=tab_words[a].rearrange("p c i -> p (c i)").bitcast(I32))
            return words

        def load_list(src, name):
            lst = sbuf([P, S // 16], U16, name)
            nc.sync.dma_start(lst[:], src)
            return lst

        def load_page(g, t, slot):
            page = sbuf([P, T2], F32, "big%d" % slot)
            nc.sync.dma_start(out=page[:], in_=page_rows[g, t])
            return page

        rounded_count = []

        def rounded_tile():
            rounded_count.append(1)
            return sbuf([P, PACK * BANK], BF16, "rounded%d" % (len(rounded_count) % 5))

        def interleave(engine_copy, src, dst=None):
            if dst is None:
                dst = rounded_tile()[:]
            engine_copy(
                out=dst.rearrange("p (c i t) -> p c t i", i=4, t=PACK),
                in_=src.rearrange("p t (c i) -> p c t i", i=4),
            )
            return dst

        def quantise(rounded, slot):
            codes = sbuf([P, BANK], U32, "codes%d" % slot)
            scales = sbuf([P, BANK], U8, "scales%d" % slot)
            nc.vector.quantize_mx(out=codes[:].bitcast(FP8X4), scales=scales[:], in_=rounded)
            return codes, scales

        tab_sc = sbuf([P, T], U8, "tab_scales")
        w2_sc = sbuf([P, GROUPS, N], U8, "w2_scales")
        nc.vector.memset(tab_sc[:].bitcast(I32), 0)
        nc.vector.memset(w2_sc[:].bitcast(I32), 0)

        w1_raw = {}
        w1_group0 = sbuf([P, K_PASSES, PACK, BANK], F32, "wide")
        tab = {}
        w1_raw[0, 0] = load_weight(w1, 0, 0, w1_group0[:, 0, :, :])
        tab[0] = load_table(0)
        list1 = load_list(offs, "list1")
        for q in range(QUADS):
            nc.scalar.dma_start(
                out=tab_sc[32 * q : 32 * q + 4 * K_PASSES, :].bitcast(I32),
                in_=tab_scales[:, 4 * q : 4 * q + 4, :].bitcast(I32),
            )
        w1_raw[1, 0] = load_weight(w1, 1, 0, w1_group0[:, 1, :, :])
        tab[1] = load_table(1)
        w1_raw[2, 0] = load_weight(w1, 2, 0, w1_group0[:, 2, :, :])
        al_sb = sbuf([P, GROUPS, PACK], F32, "al")
        nc.sync.dma_start(out=al_sb[:], in_=al.rearrange("(g p t) -> p g t", p=P, t=PACK))
        tab[2] = load_table(2)
        list2 = load_list(offs2, "list2")
        weights = {}

        def load_wgs(t0, count):
            dealt = sbuf([P, count, S], F32, "wgs%d" % t0)
            for q in QUAD_ORDER:
                nc.sync.dma_start(out=dealt[32 * q : 32 * q + 32, :, :], in_=wgs_rows[:, t0 : t0 + count, :])
            for i in range(count):
                weights[t0 + i] = dealt[:, i, :]

        load_wgs(0, 1)
        pages = {}
        pages[0, 0] = load_page(0, 0, 3)
        list3 = load_list(offs3, "list3")
        b_sb = sbuf([P, GROUPS, PACK], F32, "b")
        nc.sync.dma_start(out=b_sb[:], in_=b.rearrange("(g p t) -> p g t", p=P, t=PACK))

        picked = [sbuf([P, S], U32, "picked%d" % a) for a in range(K_PASSES)]
        picked_sc = sbuf([P, S], U8, "picked_scales")

        def quantise_w1(a, g):
            rounded = rounded_tile()
            nc.scalar.copy(
                out=rounded[:].rearrange("p (t m j) -> p m j t", t=PACK, j=PACK),
                in_=w1_raw[a, g].rearrange("p j (m t) -> p m j t", t=PACK),
            )
            return quantise(rounded[:], K_PASSES * g + a)

        def first_stage(w1_q):
            for t in range(PACK):
                for half in range(HALVES):
                    for a in range(K_PASSES):
                        codes, scales = w1_q[a]
                        nc.tensor.matmul_mx(
                            out=banks[HALVES * t + half][:],
                            lhsT=codes[:, cols(t, P)].bitcast(FP8X4),
                            lhsT_scale=scales[:, cols(t, P)],
                            rhs=picked[a][:, cols(half)].bitcast(FP8X4),
                            rhs_scale=picked_sc[4 * a : P, cols(half)],
                            start=(a == 0),
                            stop=(a == K_PASSES - 1),
                        )

        h = {}

        def features(g, t):
            for half in range(HALVES):
                bank = banks[HALVES * t + half]
                feat = h[g][:, t, cols(half)]
                nc.scalar.activation(out=feat, in_=bank[:], func=COPY, scale=al_sb[:, g, t : t + 1])
                nc.vector.tensor_tensor(out=feat, in0=bank[:], in1=feat, op=ALU.max)

        def renew(g, t):
            nc.vector.tensor_tensor(out=pages[g, t][:].indirect(list2[:]), in0=h[g][:, t, :], in1=weights[t], op=ALU.mult)

        x = {}

        def read_cells(g, t, pieces=1):
            cells = sbuf([P, S], F32, ("cells", "picked0")[t % 2])
            width = S // pieces
            for i in range(pieces):
                nc.vector.tensor_copy(out=cells[:, cols(i, width)], in_=pages[g, t][:].indirect(list3[:, cols(i, width // 16)]))
            return cells

        def add_bias(g, t, cells, span=slice(0, S)):
            nc.scalar.activation(out=x[g][:, t, span], in_=cells[:, span], func=IDENTITY, bias=b_sb[:, g, t : t + 1])

        def store_page(queue, g, t):
            queue.dma_start(out=out_rows[g, t], in_=pages[g, t][:])

        stage = {}

        def round_page(g, t, sides=(0, 1)):
            for side in sides:
                nc.scalar.copy(out=stage[g][side][:, t, :], in_=pages[g, t][:, cols(side, T2 // 2)])

        plane_sc = sbuf([P, GROUPS, T2], U8, "plane_scales")
        plane_words = [sbuf([P, T2], U32, "plane_words%d" % g) for g in range(GROUPS)]

        def planes_chunk(g, c, engine_copy, dst=None):
            rounded = interleave(engine_copy, stage[g][c // 2][:, :, cols(c % 2)], dst)
            nc.vector.quantize_mx(out=plane_words[g][:, cols(c)].bitcast(FP8X4), scales=plane_sc[:, g, cols(c)], in_=rounded)

        def store_plane_words(g, first, count):
            span = slice(first * BANK, (first + count) * BANK)
            nc.sync.dma_start(
                out=out_2[g].rearrange("p m t -> p (m t)").bitcast(I32)[:, span], in_=plane_words[g][:, span].bitcast(I32)
            )

        def store_plane_scales():
            for q in range(QUADS):
                nc.sync.dma_start(
                    out=out_3[:, 4 * q : 4 * q + 4, :].rearrange("g r c -> r g c").bitcast(I32),
                    in_=plane_sc[32 * q : 32 * q + 4, :, :].bitcast(I32),
                )

        nc.vector.tensor_copy(out=picked[0][:], in_=tab[0][:].indirect(list1[:]))
        nc.vector.tensor_copy(out=picked_sc[:], in_=tab_sc[:].indirect(list1[:]))
        w1_q = [quantise_w1(0, 0)]
        nc.vector.tensor_copy(out=picked[1][:], in_=tab[1][:].indirect(list1[:]))
        w1_q.append(quantise_w1(1, 0))
        w1_q.append(quantise_w1(2, 0))
        for half in range(HALVES):
            nc.vector.tensor_copy(out=picked[2][:, cols(half)], in_=tab[2][:].indirect(list1[:, cols(half, BANK // 16)]))
        first_stage(w1_q)

        w1_group1 = sbuf([P, K_PASSES, PACK, BANK], F32, "wide")
        w1_raw[0, 1] = load_weight(w1, 0, 1, w1_group1[:, 0, :, :])
        w1_raw[1, 1] = load_weight(w1, 1, 1, w1_group1[:, 1, :, :])
        load_wgs(1, 1)
        w1_raw[2, 1] = load_weight(w1, 2, 1, w1_group1[:, 2, :, :])
        pages[0, 1] = load_page(0, 1, 5)
        load_wgs(2, 2)
        w3_raw = [load_weight(w3, a, 0, sbuf([P, PACK, BANK], F32, "big%d" % (2, 6)[a])[:]) for a in range(GROUPS)]
        w2_w = sbuf([P, GROUPS, 2 * N], U8, "w2_words")
        nc.sync.dma_start(out=w2_w[:].bitcast(I32), in_=w2_words.rearrange("a p c -> p a c").bitcast(I32))
        for q in range(QUADS):
            nc.sync.dma_start(
                out=w2_sc[32 * q : 32 * q + 4, :, :].bitcast(I32),
                in_=w2_scales[:, 4 * q : 4 * q + 4, :].rearrange("a r c -> r a c").bitcast(I32),
            )

        h[0] = sbuf([P, PACK, S], F32, "act0")
        features(0, 0)
        renew(0, 0)
        for t in range(1, PACK):
            features(0, t)
        first_stage([quantise_w1(a, 1) for a in range(K_PASSES)])
        pages[0, 2] = load_page(0, 2, 7)
        pages[0, 3] = load_page(0, 3, 8)

        def days_scores(h_q, w3_q):
            for n in range(N // P):
                for half in range(HALVES):
                    bank = banks[HALVES * n + half]
                    for g in range(GROUPS):
                        nc.tensor.matmul_mx(
                            out=bank[:],
                            lhsT=w3_q[g][0][:, cols(n, P)].bitcast(FP8X4),
                            lhsT_scale=w3_q[g][1][:, cols(n, P)],
                            rhs=h_q[g, half][0][:].bitcast(FP8X4),
                            rhs_scale=h_q[g, half][1][:],
                            start=(g == 0),
                            stop=(g == GROUPS - 1),
                        )
                    nc.scalar.copy(out=days[n // 2][:, n % 2, cols(half)], in_=bank[:])

        def cells_pass(g, half, codes, scales):
            for n in range(N // P):
                nc.tensor.matmul_mx(
                    out=banks[HALVES * n + half][:],
                    lhsT=w2_w[:, g, cols(n, 2 * P)].bitcast(FP4X4),
                    lhsT_scale=w2_sc[:, g, cols(n, P)],
                    rhs=codes[:].bitcast(FP8X4),
                    rhs_scale=scales[:],
                    start=(g == 0),
                    stop=(g == GROUPS - 1),
                )

        def scores(half):
            for n in range(N // P):
                best = days[n // 2][:, n % 2, cols(half)]
                nc.vector.tensor_tensor(out=best, in0=banks[HALVES * n + half][:], in1=best, op=ALU.max)
                nc.sync.dma_start(out=out_0[cols(n, P), cols(half)], in_=best)

        def finish_page(g, t):
            cells = read_cells(g, t)
            store_page(nc.scalar, g, t)
            round_page(g, t)
            add_bias(g, t, cells)

        wide = sbuf([P, 4, PACK, S], BF16, "wide")
        x[0] = wide[:, 0, :, :]
        stage[0] = [wide[:, 1 + side, :, :] for side in range(2)]
        h_rounded = wide[:, 3, :, :].rearrange("p (half a) c -> p half (a c)", half=HALVES)
        h_q = {}
        h[1] = sbuf([P, PACK, S], F32, "act1")
        renew(0, 1)
        finish_page(0, 0)
        for half in range(HALVES):
            h_q[0, half] = quantise(interleave(nc.scalar.copy, h[0][:, :, cols(half)], h_rounded[:, half, :]), half)
        for t in range(PACK):
            features(1, t)
        renew(0, 2)
        finish_page(0, 1)
        w3_q = [quantise(interleave(nc.scalar.copy, w3_raw[a]), 6 + a) for a in range(GROUPS)]
        pages[1, 0] = load_page(1, 0, 2)
        pages[1, 1] = load_page(1, 1, 6)
        for half in range(HALVES):
            h_q[1, half] = quantise(interleave(nc.scalar.copy, h[1][:, :, cols(half)]), 3 + half)
        finish_page(0, 2)
        pages[1, 2] = load_page(1, 2, 7)
        renew(0, 3)
        finish_page(0, 3)
        renew(1, 0)

        held = [sbuf([P, 2, PACK * BANK], BF16, "tab_words%d" % a) for a in range(2)]
        x_q = [
            quantise(interleave(nc.scalar.copy, x[0][:, :, cols(half)]), 2 + 3 * half)
            for half in range(HALVES)
        ]
        days = [sbuf([P, 2, S], F32, ("big3", "tab_words2")[nn]) for nn in range(2)]
        days_scores(h_q, w3_q)
        for half in range(HALVES):
            cells_pass(0, half, *x_q[half])

        x[1] = sbuf([P, PACK, S], BF16, "act0")
        stage[1] = [sbuf([P, PACK, T2 // 2], BF16, "big%d" % (5, 8)[side]) for side in range(2)]
        finish_page(1, 0)
        pages[1, 3] = load_page(1, 3, 2)
        renew(1, 1)
        for c in range(T2 // BANK):
            planes_chunk(0, c, nc.scalar.copy, held[c // 2][:, c % 2, :])
        store_plane_words(0, 0, T2 // BANK)
        finish_page(1, 1)
        renew(1, 2)
        finish_page(1, 2)
        renew(1, 3)
        store_page(nc.sync, 1, 3)
        cells = read_cells(1, 3, HALVES)

        round_page(1, 3, (0,))
        add_bias(1, 3, cells, cols(0))
        cells_pass(1, 0, *quantise(interleave(nc.scalar.copy, x[1][:, :, cols(0)]), 0))
        add_bias(1, 3, cells, cols(1))
        cells_pass(1, 1, *quantise(interleave(nc.scalar.copy, x[1][:, :, cols(1)]), 1))
        round_page(1, 3, (1,))
        planes_chunk(1, 0, nc.vector.tensor_copy)
        planes_chunk(1, 1, nc.vector.tensor_copy)
        store_plane_words(1, 0, 2)
        planes_chunk(1, 2, nc.scalar.copy)
        store_plane_words(1, 2, 1)
        scores(0)
        planes_chunk(1, 3, nc.scalar.copy)
        store_plane_words(1, 3, 1)
        store_plane_scales()
        scores(1)
